import numpy as np
import ml_dtypes


def mxq(x, axis, fmt="e4m3"):
    dtype, down = {"e4m3": (ml_dtypes.float8_e4m3fn, 7), "e5m2": (ml_dtypes.float8_e5m2, 14)}[fmt]
    v = np.moveaxis(np.asarray(x, np.float32).astype(ml_dtypes.bfloat16).astype(np.float64), axis, -1)
    blocks = v.reshape(v.shape[:-1] + (-1, 32))
    amax = np.abs(blocks).max(-1, keepdims=True)
    byte = np.maximum(np.where(amax > 0, np.frexp(amax)[1] - 1 + 127, 0) - down, 1)
    scale = np.exp2(byte - 127.0)
    codes = (blocks / scale).astype(np.float32).astype(dtype).astype(np.float64)
    return np.moveaxis((codes * scale).reshape(v.shape), -1, axis)


WIDE = False


def mx_kscale(k):
    if not WIDE:
        return np.ones(k)
    levels = np.array([10, -10, 5, -5, 0])
    if k % 512:
        return np.exp2(np.random.permutation(np.resize(levels, k // 32))).repeat(32)
    a = np.empty((k // 512, 16))
    for p in range(k // 512):
        a[p, :8] = np.random.permutation(np.resize(levels, 8))
        for g in range(8):
            far = levels[np.abs(levels - a[p, g]) >= 10]
            a[p, g + 8] = far[np.random.randint(len(far))]
    return np.exp2(a.ravel()).repeat(32)


def f64(x):
    return np.asarray(x).astype(np.float64)


def striped(idx):
    return np.tile(idx.reshape(-1, 16).T, (8, 1)).astype(np.uint16)


def unstriped(offs):
    return offs[:16].T.reshape(-1).astype(np.int64)


E2M1 = np.array([0.0, 0.5, 1.0, 1.5, 2.0, 3.0, 4.0, 6.0, -0.0, -0.5, -1.0, -1.5, -2.0, -3.0, -4.0, -6.0])


def pack_weight(w, fmt):
    k, n = w.shape
    w = f64(np.asarray(w, np.float32).astype(ml_dtypes.bfloat16)).reshape(k // 32, 32, n)
    amax = np.abs(w).max(1)
    if fmt == "e4m3":
        byte = np.frexp(amax)[1] - 1 + 127 - 7
    else:
        mant, ex = np.frexp(amax / 6.0)
        byte = np.where(mant > 0.5, ex, ex - 1) + 127
    byte = np.clip(np.where(amax > 0, byte, 1), 1, 254)
    scaled = (w * np.exp2(127.0 - byte)[:, None, :]).reshape(k, n).astype(np.float32)
    by_word = np.ascontiguousarray(scaled.reshape(k // 512, 128, 4, n).transpose(0, 1, 3, 2))
    if fmt == "e4m3":
        words = by_word.astype(ml_dtypes.float8_e4m3fn).view(np.uint8)
    else:
        c = by_word.astype(ml_dtypes.float4_e2m1fn).view(np.uint8) & 0xF
        words = (c[..., 0::2] | (c[..., 1::2] << 4)).reshape(k // 512, 128, 2 * n)
    return np.ascontiguousarray(words), np.ascontiguousarray(byte.astype(np.uint8).reshape(k // 512, 16, n))


def unpack_weight(words, scales, fmt):
    g, _, n = scales.shape
    words = np.ascontiguousarray(words).reshape(g, 128, n, -1)
    if fmt == "e4m3":
        vals = words.view(ml_dtypes.float8_e4m3fn).astype(np.float64)
    else:
        nib = np.empty((g, 128, n, 4), np.uint8)
        nib[..., 0::2] = words & 0xF
        nib[..., 1::2] = words >> 4
        vals = E2M1[nib]
    vals = vals * np.repeat(np.exp2(scales.astype(np.float64) - 127.0), 8, axis=1)[..., None]
    return vals.transpose(0, 1, 3, 2).reshape(g * 512, n)


def gelu(v):
    return 0.5 * v * (1.0 + np.tanh(np.sqrt(2.0 / np.pi) * (v + 0.044715 * v**3)))


K, K1, T, H, S, T3, S2 = 2048, 1024, 2048, 1024, 512, 1024, 512

def setup_inputs():
    n = np.random.standard_normal
    s = mx_kscale(K)[:, None]
    u = mx_kscale(H)[:, None]
    tab_words, tab_scales = pack_weight(n((K, T)) * s, "e4m3")
    tab2_words, tab2_scales = pack_weight(n((H, T3)) / u / np.sqrt(H), "e4m3")
    tab3_words, tab3_scales = pack_weight(n((H, T3)) / u / np.sqrt(H), "e4m3")
    w4_words, w4_scales = pack_weight(1.6 * n((K1, H)) / s[:K1] / np.sqrt(K), "e2m1")
    return {
        "tab_words": tab_words, "tab_scales": tab_scales,
        "tab2_words": tab2_words, "tab2_scales": tab2_scales,
        "tab3_words": tab3_words, "tab3_scales": tab3_scales,
        "offs": striped(np.random.permutation(T)[:S]),
        "offs2": striped(np.random.permutation(T3)[:S2]),
        "offs3": striped(np.random.permutation(T3)[:S2]),
        "w4_words": w4_words, "w4_scales": w4_scales,
        "w1": (1.6 * n((K - K1, H)) / s[K1:] / np.sqrt(K)).astype(np.float32),
        "gain": (np.exp(0.3 * n(H)) * u[:, 0]).astype(np.float32),
        "lean": (0.6 * n(S2)).astype(np.float32),
        "weight": np.exp(0.4 * n(S2)).astype(np.float32),
    }

def reference(tab_words, tab_scales, tab2_words, tab2_scales, tab3_words, tab3_scales,
              offs, offs2, offs3, w4_words, w4_scales, w1, gain, lean, weight):
    v = unpack_weight(tab_words, tab_scales, "e4m3")[:, unstriped(offs)]
    v2 = unpack_weight(tab2_words, tab2_scales, "e4m3")[:, unstriped(offs2)]
    v3 = unpack_weight(tab3_words, tab3_scales, "e4m3")[:, unstriped(offs3)]
    w4 = unpack_weight(w4_words, w4_scales, "e2m1")
    w1q = mxq(f64(w1), 0, "e4m3")
    z = w4.T @ v[:K1] + w1q.T @ v[K1:]
    h = z / (1.0 + np.exp(-z)) * f64(gain)[:, None]
    hq = mxq(h, 0, "e4m3")
    e = v2.T @ hq + v3.T @ hq
    return np.tanh(e + f64(lean)[:, None]) * f64(weight)[:, None]

@@ -1,0 +1,241 @@
+from contextlib import ExitStack
+
+import concourse.mybir as mybir
+
+F32 = mybir.dt.float32
+BF16 = mybir.dt.bfloat16
+I32 = mybir.dt.int32
+U32 = mybir.dt.uint32
+U16 = mybir.dt.uint16
+U8 = mybir.dt.uint8
+FP8X4 = mybir.dt.float8_e4m3fn_x4
+FP4X4 = mybir.dt.float4_e2m1fn_x4
+ACT = mybir.ActivationFunctionType
+ALU = mybir.AluOpType
+
+P = 128
+PACK = 4
+K_PASS = P * PACK
+T, H, S, T3, S2 = 2048, 1024, 512, 1024, 512
+BLOCKS = H // K_PASS
+JQ = 128
+JH = 256
+
+FLOPS = 2 * 2048 * H * S + 2 * 2 * H * S2 * S
+
+
+def tile_list_homeshare_trio_scores_kernel(
+    tc, tab_words, tab_scales, tab2_words, tab2_scales, tab3_words, tab3_scales,
+    offs, offs2, offs3, w4_words, w4_scales, w1, gain, lean, weight, out,
+):
+    nc = tc.nc
+    with ExitStack() as ctx:
+        sb = ctx.enter_context(tc.tile_pool(name="sb", bufs=1))
+        psum = ctx.enter_context(tc.psum_pool(name="psum", bufs=1))
+
+        def tile(name, shape, dtype):
+            return sb.tile(shape, dtype, name=name, align_bytes=64)
+
+        def zeroed(name, shape):
+            t = tile(name, shape, U8)
+            nc.vector.memset(t[:].bitcast(I32), 0)
+            return t
+
+        def load_list(name, src):
+            t = sb.tile([P, S // 16], U16, name=name)
+            nc.sync.dma_start(t[:], src)
+            return t
+
+        def load_words(name, src):
+            t = tile(name, [P, src.shape[1]], U32)
+            nc.sync.dma_start(t[:].bitcast(I32), src.rearrange("p n t -> p (n t)").bitcast(I32))
+            return t
+
+        def load_packed_scales(dst, src):
+            passes = src.shape[0]
+            for q in range(4):
+                nc.sync.dma_start(
+                    dst[32 * q : 32 * q + 4 * passes, :].bitcast(I32),
+                    src[:, 4 * q : 4 * q + 4, :].bitcast(I32),
+                )
+
+        def load_w1(a, b, h, n):
+            width = K_PASS // n
+            t = tile(f"w1raw{a}{b}{h}", [P, PACK, width], F32)
+            c0 = K_PASS * b + width * h
+            rows = w1[K_PASS * a : K_PASS * (a + 1), c0 : c0 + width]
+            nc.sync.dma_start(t[:], rows.rearrange("(p i) c -> p i c", i=PACK))
+            return t
+
+        def gather(name, window, lst, dtype):
+            g = tile(name, [P, S], dtype)
+            nc.vector.tensor_copy(g[:], window[:].indirect(lst[:]))
+            return g
+
+        tabs_raw = zeroed("tabs_raw", [P, T])
+        w4s_raw = zeroed("w4s_raw", [P, 2 * H])
+        t2s_raw = zeroed("t2s_raw", [P, T3])
+        t3s_raw = zeroed("t3s_raw", [P, T3])
+        vs1 = zeroed("vs1", [P, S])
+
+        idx = load_list("idx", offs)
+        w4_raw = tile("w4_raw", [P, 2, 2 * H], U8)
+        nc.sync.dma_start(w4_raw[:].bitcast(I32), w4_words.rearrange("a p c -> p a c").bitcast(I32))
+        load_packed_scales(tabs_raw, tab_scales)
+        tab = [load_words("tab0", tab_words[0])]
+        idx2 = load_list("idx2", offs2)
+        for q in range(4):
+            nc.sync.dma_start(
+                w4s_raw[32 * q : 32 * q + 4, :].rearrange("p (a c) -> p a c", a=2).bitcast(I32),
+                w4_scales[:, 4 * q : 4 * q + 4, :].rearrange("a r c -> r a c").bitcast(I32),
+            )
+        w1_raw = {}
+        w1_raw[0, 0] = [load_w1(0, 0, 0, 1)]
+        load_packed_scales(t2s_raw, tab2_scales)
+        tab.append(load_words("tab1", tab_words[1]))
+        idx3 = load_list("idx3", offs3)
+        load_packed_scales(t3s_raw, tab3_scales)
+        w1_raw[1, 0] = [load_w1(1, 0, 0, 1)]
+        gain_sb = tile("gain_sb", [P, BLOCKS, PACK], F32)
+        nc.sync.dma_start(gain_sb[:], gain.rearrange("(b p t) -> p b t", p=P, t=PACK))
+        tab.append(load_words("tab2", tab_words[2]))
+        lean_sb = tile("lean_sb", [P, 4], F32)
+        weight_sb = tile("weight_sb", [P, 4], F32)
+        with nc.allow_non_contiguous_dma(reason="one value a partition"):
+            nc.sync.dma_start(lean_sb[:], lean.rearrange("(c p) -> p c", p=P))
+            nc.sync.dma_start(weight_sb[:], weight.rearrange("(c p) -> p c", p=P))
+        tab.append(load_words("tab3", tab_words[3]))
+        lodger = [load_words("lodger0", tab2_words[0])]
+        w1_raw[0, 1] = [load_w1(0, 1, 0, 1)]
+        volunteer = [load_words("volunteer0", tab3_words[0])]
+        w1_raw[1, 1] = [load_w1(1, 1, h, 2) for h in range(2)]
+        lodger.append(load_words("lodger1", tab2_words[1]))
+        volunteer.append(load_words("volunteer1", tab3_words[1]))
+
+        vs = gather("vs", tabs_raw, idx, U8)
+        nc.scalar.dma_start(vs1[0:100, :].bitcast(I32), vs[4:104, :].bitcast(I32))
+
+        w4 = tile("w4", [P, 2 * 2 * H], U8)
+        nc.vector.tensor_copy(
+            w4[:].bitcast(U16).rearrange("p (g t m) -> p g m t", t=PACK, m=P),
+            w4_raw[:].rearrange("p a c -> p (a c)").bitcast(U16).rearrange("p (g m t) -> p g m t", t=PACK, m=P),
+        )
+        v0 = gather("v0", tab[0], idx, U32)
+        w4s = tile("w4s", [P, 2 * H], U8)
+        nc.vector.tensor_copy(
+            w4s[:].rearrange("p (g t m) -> p g m t", t=PACK, m=P),
+            w4s_raw[:].rearrange("p (g m t) -> p g m t", t=PACK, m=P),
+        )
+
+        z = [[psum.tile([P, PACK, JQ], F32, name=f"z{b}{q}", tag=f"bank{b}{q}") for q in range(4)] for b in range(BLOCKS)]
+
+        def z_pass(a, b, v, v_scale, weights):
+            for q in range(4):
+                cols = slice(JQ * q, JQ * (q + 1))
+                for t in range(PACK):
+                    lhs, lhs_scale = weights(t)
+                    nc.tensor.matmul_mx(
+                        out=z[b][q][:, t, :], lhsT=lhs, lhsT_scale=lhs_scale,
+                        rhs=v[:, cols].bitcast(FP8X4), rhs_scale=v_scale[:, cols],
+                        start=(a == 0 and t == 0), stop=(a == 3 and t == PACK - 1),
+                    )
+
+        def w4_weights(a, b):
+            def get(t):
+                c0 = H * a + K_PASS * b + P * t
+                return w4[:, 2 * c0 : 2 * (c0 + P)].bitcast(FP4X4), w4s[:, c0 : c0 + P]
+            return get
+
+        def w1_weights(a, b):
+            grouped = tile(f"w1bf{a}{b}", [P, PACK, P, PACK], BF16)
+            pieces = w1_raw[a, b]
+            mw = P // len(pieces)
+            for h, raw in enumerate(pieces):
+                nc.scalar.copy(
+                    grouped[:, :, mw * h : mw * (h + 1), :].rearrange("p t m i -> p m i t"),
+                    raw[:].rearrange("p i (m t) -> p m i t", t=PACK),
+                )
+            codes = tile(f"w1q{a}{b}", [P, K_PASS], U32)
+            scales = tile(f"w1s{a}{b}", [P, K_PASS], U8)
+            for tp in range(2):
+                nc.vector.quantize_mx(
+                    out=codes[:, 256 * tp : 256 * (tp + 1)].bitcast(FP8X4),
+                    scales=scales[:, 256 * tp : 256 * (tp + 1)],
+                    in_=grouped[:, 2 * tp : 2 * tp + 2, :, :].rearrange("p t m i -> p (t m i)"),
+                )
+
+            def get(t):
+                return codes[:, P * t : P * (t + 1)].bitcast(FP8X4), scales[:, P * t : P * (t + 1)]
+            return get
+
+        hq = [tile(f"hq{b}", [P, S], U32) for b in range(BLOCKS)]
+        hs = [tile(f"hs{b}", [P, S], U8) for b in range(BLOCKS)]
+
+        def make_h(b, q):
+            act = tile(f"silu{b}{q}", [P, JQ, PACK], F32)
+            nc.scalar.activation(act[:], z[b][q][:].rearrange("p t j -> p j t"), ACT.Silu)
+            hb = tile(f"hb{b}{q}", [P, JQ, PACK], BF16)
+            nc.vector.tensor_tensor(
+                hb[:], act[:], gain_sb[:, b, :].unsqueeze(1).to_broadcast([P, JQ, PACK]), ALU.mult
+            )
+            cols = slice(JQ * q, JQ * (q + 1))
+            nc.vector.quantize_mx(
+                out=hq[b][:, cols].bitcast(FP8X4), scales=hs[b][:, cols], in_=hb[:].rearrange("p j t -> p (j t)")
+            )
+
+        for b in range(BLOCKS):
+            z_pass(0, b, v0, vs, w4_weights(0, b))
+        g2s = gather("g2s", t2s_raw, idx2, U8)
+        w1_00 = w1_weights(0, 0)
+        v1 = gather("v1", tab[1], idx, U32)
+        for b in range(BLOCKS):
+            z_pass(1, b, v1, vs1, w4_weights(1, b))
+        g3s = gather("g3s", t3s_raw, idx3, U8)
+        w1_10 = w1_weights(1, 0)
+        v2 = gather("v2", tab[2], idx, U32)
+        z_pass(2, 0, v2, vs[8:P, :], w1_00)
+        v3 = gather("v3", tab[3], idx, U32)
+        z_pass(3, 0, v3, vs[12:P, :], w1_10)
+        g2 = [gather("g20", lodger[0], idx2, U32)]
+        for q in range(4):
+            make_h(0, q)
+        g3 = [gather("g30", volunteer[0], idx3, U32)]
+        z_pass(2, 1, v2, vs[8:P, :], w1_weights(0, 1))
+
+        e = [[psum.tile([P, 2, JH], F32, name=f"e{jh}{mp}", tag=f"bank0{2 * jh + mp}") for mp in range(2)] for jh in range(2)]
+
+        def e_pass(b, jh, mp):
+            cols = slice(JH * jh, JH * (jh + 1))
+            for n, (g, gs) in enumerate(((g2[b], g2s), (g3[b], g3s))):
+                for u in range(2):
+                    m0 = P * (2 * mp + u)
+                    nc.tensor.matmul_mx(
+                        out=e[jh][mp][:, u, :],
+                        lhsT=g[:, m0 : m0 + P].bitcast(FP8X4), lhsT_scale=gs[4 * b : P, m0 : m0 + P],
+                        rhs=hq[b][:, cols].bitcast(FP8X4), rhs_scale=hs[b][:, cols],
+                        start=(b == 0 and n == 0 and u == 0), stop=(b == 1 and n == 1 and u == 1),
+                    )
+
+        for jh in range(2):
+            for mp in range(2):
+                e_pass(0, jh, mp)
+        z_pass(3, 1, v3, vs[12:P, :], w1_weights(1, 1))
+        g2.append(gather("g21", lodger[1], idx2, U32))
+        for q in range(2):
+            make_h(1, q)
+        g3.append(gather("g31", volunteer[1], idx3, U32))
+        for q in range(2, 4):
+            make_h(1, q)
+        for jh in range(2):
+            for mp in range(2):
+                e_pass(1, jh, mp)
+                th = tile(f"th{jh}{mp}", [P, 2, JH], F32)
+                res = tile(f"res{jh}{mp}", [P, 2, JH], F32)
+                for u in range(2):
+                    c = 2 * mp + u
+                    nc.scalar.activation(th[:, u, :], e[jh][mp][:, u, :], ACT.Tanh, bias=lean_sb[:, c : c + 1])
+                    nc.vector.tensor_scalar(
+                        res[:, u, :], th[:, u, :], weight_sb[:, c : c + 1], None, ALU.mult
+                    )
+                rows = out[2 * P * mp : 2 * P * (mp + 1), JH * jh : JH * (jh + 1)]
+                nc.sync.dma_start(rows.rearrange("(u p) j -> p u j", p=P), res[:])

@@ -51,10 +51,10 @@ def tile_list_homeshare_trio_scores_kernel(
             nc.sync.dma_start(t[:].bitcast(I32), src.rearrange("p n t -> p (n t)").bitcast(I32))
             return t
 
-        def load_packed_scales(dst, src):
+        def load_packed_scales(queue, dst, src):
             passes = src.shape[0]
             for q in range(4):
-                nc.sync.dma_start(
+                queue.dma_start(
                     dst[32 * q : 32 * q + 4 * passes, :].bitcast(I32),
                     src[:, 4 * q : 4 * q + 4, :].bitcast(I32),
                 )
@@ -79,31 +79,31 @@ def tile_list_homeshare_trio_scores_kernel(
         vs1 = zeroed("vs1", [P, S])
 
         idx = load_list("idx", offs)
+        idx2 = load_list("idx2", offs2)
+        load_packed_scales(nc.sync, tabs_raw, tab_scales)
         w4_raw = tile("w4_raw", [P, 2, 2 * H], U8)
         nc.sync.dma_start(w4_raw[:].bitcast(I32), w4_words.rearrange("a p c -> p a c").bitcast(I32))
-        load_packed_scales(tabs_raw, tab_scales)
         tab = [load_words("tab0", tab_words[0])]
-        idx2 = load_list("idx2", offs2)
         for q in range(4):
             nc.sync.dma_start(
                 w4s_raw[32 * q : 32 * q + 4, :].rearrange("p (a c) -> p a c", a=2).bitcast(I32),
                 w4_scales[:, 4 * q : 4 * q + 4, :].rearrange("a r c -> r a c").bitcast(I32),
             )
-        w1_raw = {}
-        w1_raw[0, 0] = [load_w1(0, 0, 0, 1)]
-        load_packed_scales(t2s_raw, tab2_scales)
-        tab.append(load_words("tab1", tab_words[1]))
         idx3 = load_list("idx3", offs3)
-        load_packed_scales(t3s_raw, tab3_scales)
-        w1_raw[1, 0] = [load_w1(1, 0, 0, 1)]
         gain_sb = tile("gain_sb", [P, BLOCKS, PACK], F32)
         nc.sync.dma_start(gain_sb[:], gain.rearrange("(b p t) -> p b t", p=P, t=PACK))
-        tab.append(load_words("tab2", tab_words[2]))
+        w1_raw = {}
+        w1_raw[0, 0] = [load_w1(0, 0, 0, 1)]
+        tab.append(load_words("tab1", tab_words[1]))
+        load_packed_scales(nc.sync, t2s_raw, tab2_scales)
         lean_sb = tile("lean_sb", [P, 4], F32)
         weight_sb = tile("weight_sb", [P, 4], F32)
         with nc.allow_non_contiguous_dma(reason="one value a partition"):
             nc.sync.dma_start(lean_sb[:], lean.rearrange("(c p) -> p c", p=P))
             nc.sync.dma_start(weight_sb[:], weight.rearrange("(c p) -> p c", p=P))
+        w1_raw[1, 0] = [load_w1(1, 0, 0, 1)]
+        tab.append(load_words("tab2", tab_words[2]))
+        load_packed_scales(nc.sync, t3s_raw, tab3_scales)
         tab.append(load_words("tab3", tab_words[3]))
         lodger = [load_words("lodger0", tab2_words[0])]
         w1_raw[0, 1] = [load_w1(0, 1, 0, 1)]
@@ -113,18 +113,18 @@ def tile_list_homeshare_trio_scores_kernel(
         volunteer.append(load_words("volunteer1", tab3_words[1]))
 
         vs = gather("vs", tabs_raw, idx, U8)
-        nc.scalar.dma_start(vs1[0:100, :].bitcast(I32), vs[4:104, :].bitcast(I32))
+        nc.gpsimd.dma_start(vs1[0:100, :].bitcast(I32), vs[4:104, :].bitcast(I32))
 
         w4 = tile("w4", [P, 2 * 2 * H], U8)
         nc.vector.tensor_copy(
-            w4[:].bitcast(U16).rearrange("p (g t m) -> p g m t", t=PACK, m=P),
-            w4_raw[:].rearrange("p a c -> p (a c)").bitcast(U16).rearrange("p (g m t) -> p g m t", t=PACK, m=P),
+            w4[:].bitcast(U16).rearrange("p (g t m) -> p g t m", t=PACK, m=P),
+            w4_raw[:].rearrange("p a c -> p (a c)").bitcast(U16).rearrange("p (g m t) -> p g t m", t=PACK, m=P),
         )
         v0 = gather("v0", tab[0], idx, U32)
         w4s = tile("w4s", [P, 2 * H], U8)
         nc.vector.tensor_copy(
-            w4s[:].rearrange("p (g t m) -> p g m t", t=PACK, m=P),
-            w4s_raw[:].rearrange("p (g m t) -> p g m t", t=PACK, m=P),
+            w4s[:].rearrange("p (g t m) -> p g t m", t=PACK, m=P),
+            w4s_raw[:].rearrange("p (g m t) -> p g t m", t=PACK, m=P),
         )
 
         z = [[psum.tile([P, PACK, JQ], F32, name=f"z{b}{q}", tag=f"bank{b}{q}") for q in range(4)] for b in range(BLOCKS)]
@@ -152,8 +152,8 @@ def tile_list_homeshare_trio_scores_kernel(
             mw = P // len(pieces)
             for h, raw in enumerate(pieces):
                 nc.scalar.copy(
-                    grouped[:, :, mw * h : mw * (h + 1), :].rearrange("p t m i -> p m i t"),
-                    raw[:].rearrange("p i (m t) -> p m i t", t=PACK),
+                    grouped[:, :, mw * h : mw * (h + 1), :].rearrange("p t m i -> p m t i"),
+                    raw[:].rearrange("p i (m t) -> p m t i", t=PACK),
                 )
             codes = tile(f"w1q{a}{b}", [P, K_PASS], U32)
             scales = tile(f"w1s{a}{b}", [P, K_PASS], U8)
@@ -171,34 +171,36 @@ def tile_list_homeshare_trio_scores_kernel(
         hq = [tile(f"hq{b}", [P, S], U32) for b in range(BLOCKS)]
         hs = [tile(f"hs{b}", [P, S], U8) for b in range(BLOCKS)]
 
-        def make_h(b, q):
-            act = tile(f"silu{b}{q}", [P, JQ, PACK], F32)
-            nc.scalar.activation(act[:], z[b][q][:].rearrange("p t j -> p j t"), ACT.Silu)
-            hb = tile(f"hb{b}{q}", [P, JQ, PACK], BF16)
-            nc.vector.tensor_tensor(
-                hb[:], act[:], gain_sb[:, b, :].unsqueeze(1).to_broadcast([P, JQ, PACK]), ALU.mult
-            )
-            cols = slice(JQ * q, JQ * (q + 1))
+        def make_h(b, jh):
+            hb = tile(f"hb{b}{jh}", [P, 2, JQ, PACK], BF16)
+            for u in range(2):
+                q = 2 * jh + u
+                act = tile(f"silu{b}{q}", [P, JQ, PACK], F32)
+                nc.scalar.activation(act[:], z[b][q][:].rearrange("p t j -> p j t"), ACT.Silu)
+                nc.vector.tensor_tensor(
+                    hb[:, u, :, :], act[:], gain_sb[:, b, :].unsqueeze(1).to_broadcast([P, JQ, PACK]), ALU.mult
+                )
+            cols = slice(JH * jh, JH * (jh + 1))
             nc.vector.quantize_mx(
-                out=hq[b][:, cols].bitcast(FP8X4), scales=hs[b][:, cols], in_=hb[:].rearrange("p j t -> p (j t)")
+                out=hq[b][:, cols].bitcast(FP8X4), scales=hs[b][:, cols], in_=hb[:].rearrange("p u j t -> p (u j t)")
             )
 
         for b in range(BLOCKS):
             z_pass(0, b, v0, vs, w4_weights(0, b))
-        g2s = gather("g2s", t2s_raw, idx2, U8)
         w1_00 = w1_weights(0, 0)
         v1 = gather("v1", tab[1], idx, U32)
         for b in range(BLOCKS):
             z_pass(1, b, v1, vs1, w4_weights(1, b))
-        g3s = gather("g3s", t3s_raw, idx3, U8)
+        g2s = gather("g2s", t2s_raw, idx2, U8)
         w1_10 = w1_weights(1, 0)
         v2 = gather("v2", tab[2], idx, U32)
         z_pass(2, 0, v2, vs[8:P, :], w1_00)
+        g3s = gather("g3s", t3s_raw, idx3, U8)
         v3 = gather("v3", tab[3], idx, U32)
         z_pass(3, 0, v3, vs[12:P, :], w1_10)
         g2 = [gather("g20", lodger[0], idx2, U32)]
-        for q in range(4):
-            make_h(0, q)
+        for jh in range(2):
+            make_h(0, jh)
         g3 = [gather("g30", volunteer[0], idx3, U32)]
         z_pass(2, 1, v2, vs[8:P, :], w1_weights(0, 1))
 
@@ -221,11 +223,9 @@ def tile_list_homeshare_trio_scores_kernel(
                 e_pass(0, jh, mp)
         z_pass(3, 1, v3, vs[12:P, :], w1_weights(1, 1))
         g2.append(gather("g21", lodger[1], idx2, U32))
-        for q in range(2):
-            make_h(1, q)
         g3.append(gather("g31", volunteer[1], idx3, U32))
-        for q in range(2, 4):
-            make_h(1, q)
+        for jh in range(2):
+            make_h(1, jh)
         for jh in range(2):
             for mp in range(2):
                 e_pass(1, jh, mp)

@@ -67,65 +67,71 @@ def tile_list_homeshare_trio_scores_kernel(
             nc.sync.dma_start(t[:], rows.rearrange("(p i) c -> p i c", i=PACK))
             return t
 
-        def gather(name, window, lst, dtype):
-            g = tile(name, [P, S], dtype)
-            nc.vector.tensor_copy(g[:], window[:].indirect(lst[:]))
+        def gather(name, window, lst, dtype, tag=None, pieces=1):
+            g = sb.tile([P, S], dtype, name=name, tag=tag or name, align_bytes=64)
+            n = S // pieces
+            for h in range(pieces):
+                offsets = lst[:, n // 16 * h : n // 16 * (h + 1)]
+                nc.vector.tensor_copy(g[:, n * h : n * (h + 1)], window[:].indirect(offsets))
             return g
 
         tabs_raw = zeroed("tabs_raw", [P, T])
-        w4s_raw = zeroed("w4s_raw", [P, 2 * H])
         t2s_raw = zeroed("t2s_raw", [P, T3])
         t3s_raw = zeroed("t3s_raw", [P, T3])
+        w4s_raw = zeroed("w4s_raw", [P, 2 * H])
         vs1 = zeroed("vs1", [P, S])
 
-        idx = load_list("idx", offs)
-        idx2 = load_list("idx2", offs2)
-        load_packed_scales(nc.sync, tabs_raw, tab_scales)
         w4_raw = tile("w4_raw", [P, 2, 2 * H], U8)
         nc.sync.dma_start(w4_raw[:].bitcast(I32), w4_words.rearrange("a p c -> p a c").bitcast(I32))
+        idx = load_list("idx", offs)
         tab = [load_words("tab0", tab_words[0])]
+        load_packed_scales(nc.sync, tabs_raw, tab_scales)
+        w1_raw = {}
+        w1_raw[0, 0] = [load_w1(0, 0, 0, 1)]
+        idx2 = load_list("idx2", offs2)
+        idx3 = load_list("idx3", offs3)
+        tab.append(load_words("tab1", tab_words[1]))
         for q in range(4):
             nc.sync.dma_start(
                 w4s_raw[32 * q : 32 * q + 4, :].rearrange("p (a c) -> p a c", a=2).bitcast(I32),
                 w4_scales[:, 4 * q : 4 * q + 4, :].rearrange("a r c -> r a c").bitcast(I32),
             )
-        idx3 = load_list("idx3", offs3)
-        gain_sb = tile("gain_sb", [P, BLOCKS, PACK], F32)
-        nc.sync.dma_start(gain_sb[:], gain.rearrange("(b p t) -> p b t", p=P, t=PACK))
-        w1_raw = {}
-        w1_raw[0, 0] = [load_w1(0, 0, 0, 1)]
-        tab.append(load_words("tab1", tab_words[1]))
-        load_packed_scales(nc.sync, t2s_raw, tab2_scales)
-        lean_sb = tile("lean_sb", [P, 4], F32)
-        weight_sb = tile("weight_sb", [P, 4], F32)
-        with nc.allow_non_contiguous_dma(reason="one value a partition"):
-            nc.sync.dma_start(lean_sb[:], lean.rearrange("(c p) -> p c", p=P))
-            nc.sync.dma_start(weight_sb[:], weight.rearrange("(c p) -> p c", p=P))
         w1_raw[1, 0] = [load_w1(1, 0, 0, 1)]
         tab.append(load_words("tab2", tab_words[2]))
-        load_packed_scales(nc.sync, t3s_raw, tab3_scales)
         tab.append(load_words("tab3", tab_words[3]))
+        gain_sb = tile("gain_sb", [P, BLOCKS, PACK], F32)
+        nc.sync.dma_start(gain_sb[:], gain.rearrange("(b p t) -> p b t", p=P, t=PACK))
         lodger = [load_words("lodger0", tab2_words[0])]
         w1_raw[0, 1] = [load_w1(0, 1, 0, 1)]
         volunteer = [load_words("volunteer0", tab3_words[0])]
         w1_raw[1, 1] = [load_w1(1, 1, h, 2) for h in range(2)]
         lodger.append(load_words("lodger1", tab2_words[1]))
         volunteer.append(load_words("volunteer1", tab3_words[1]))
+        lean_sb = tile("lean_sb", [P, 4], F32)
+        weight_sb = tile("weight_sb", [P, 4], F32)
+        with nc.allow_non_contiguous_dma(reason="one value a partition"):
+            nc.sync.dma_start(lean_sb[:], lean.rearrange("(c p) -> p c", p=P))
+            nc.sync.dma_start(weight_sb[:], weight.rearrange("(c p) -> p c", p=P))
 
+
+        load_packed_scales(nc.gpsimd, t2s_raw, tab2_scales)
+        load_packed_scales(nc.gpsimd, t3s_raw, tab3_scales)
+
+        def deal_columns(name, raw, b, dtype):
+            dealt = tile(name, [P, 2, PACK, P], dtype)
+            src = raw.rearrange("p (a b m t) -> p a b t m", a=2, b=BLOCKS, t=PACK)
+            nc.vector.tensor_copy(dealt[:], src[:, :, b, :, :])
+            return dealt
+
+        w4_u16 = w4_raw[:].rearrange("p a c -> p (a c)").bitcast(U16)
+        w4 = [deal_columns(f"w4_{b}", w4_u16, b, U16) for b in range(BLOCKS)]
+        v0 = gather("v0", tab[0], idx, U32)
         vs = gather("vs", tabs_raw, idx, U8)
         nc.gpsimd.dma_start(vs1[0:100, :].bitcast(I32), vs[4:104, :].bitcast(I32))
-
-        w4 = tile("w4", [P, 2 * 2 * H], U8)
-        nc.vector.tensor_copy(
-            w4[:].bitcast(U16).rearrange("p (g t m) -> p g t m", t=PACK, m=P),
-            w4_raw[:].rearrange("p a c -> p (a c)").bitcast(U16).rearrange("p (g m t) -> p g t m", t=PACK, m=P),
-        )
-        v0 = gather("v0", tab[0], idx, U32)
-        w4s = tile("w4s", [P, 2 * H], U8)
-        nc.vector.tensor_copy(
-            w4s[:].rearrange("p (g t m) -> p g t m", t=PACK, m=P),
-            w4s_raw[:].rearrange("p (g m t) -> p g t m", t=PACK, m=P),
-        )
+        g2s = gather("g2s", t2s_raw, idx2, U8, tag="tabs_raw")
+        g3s = gather("g3s", t3s_raw, idx3, U8, tag="t2s_raw")
+        v1 = gather("v1", tab[1], idx, U32)
+        w4s = [deal_columns(f"w4s_{b}", w4s_raw[:], b, U8) for b in range(BLOCKS)]
 
         z = [[psum.tile([P, PACK, JQ], F32, name=f"z{b}{q}", tag=f"bank{b}{q}") for q in range(4)] for b in range(BLOCKS)]
 
@@ -142,8 +148,7 @@ def tile_list_homeshare_trio_scores_kernel(
 
         def w4_weights(a, b):
             def get(t):
-                c0 = H * a + K_PASS * b + P * t
-                return w4[:, 2 * c0 : 2 * (c0 + P)].bitcast(FP4X4), w4s[:, c0 : c0 + P]
+                return w4[b][:, a, t, :].bitcast(FP4X4), w4s[b][:, a, t, :]
             return get
 
         def w1_weights(a, b):
@@ -152,8 +157,8 @@ def tile_list_homeshare_trio_scores_kernel(
             mw = P // len(pieces)
             for h, raw in enumerate(pieces):
                 nc.scalar.copy(
-                    grouped[:, :, mw * h : mw * (h + 1), :].rearrange("p t m i -> p m t i"),
-                    raw[:].rearrange("p i (m t) -> p m t i", t=PACK),
+                    grouped[:, :, mw * h : mw * (h + 1), :].rearrange("p t m i -> p m i t"),
+                    raw[:].rearrange("p i (m t) -> p m i t", t=PACK),
                 )
             codes = tile(f"w1q{a}{b}", [P, K_PASS], U32)
             scales = tile(f"w1s{a}{b}", [P, K_PASS], U8)
@@ -185,19 +190,16 @@ def tile_list_homeshare_trio_scores_kernel(
                 out=hq[b][:, cols].bitcast(FP8X4), scales=hs[b][:, cols], in_=hb[:].rearrange("p u j t -> p (u j t)")
             )
 
-        for b in range(BLOCKS):
-            z_pass(0, b, v0, vs, w4_weights(0, b))
+        z_pass(0, 0, v0, vs, w4_weights(0, 0))
+        z_pass(1, 0, v1, vs1, w4_weights(1, 0))
         w1_00 = w1_weights(0, 0)
-        v1 = gather("v1", tab[1], idx, U32)
-        for b in range(BLOCKS):
-            z_pass(1, b, v1, vs1, w4_weights(1, b))
-        g2s = gather("g2s", t2s_raw, idx2, U8)
         w1_10 = w1_weights(1, 0)
         v2 = gather("v2", tab[2], idx, U32)
         z_pass(2, 0, v2, vs[8:P, :], w1_00)
-        g3s = gather("g3s", t3s_raw, idx3, U8)
-        v3 = gather("v3", tab[3], idx, U32)
+        v3 = gather("v3", tab[3], idx, U32, pieces=2)
         z_pass(3, 0, v3, vs[12:P, :], w1_10)
+        z_pass(0, 1, v0, vs, w4_weights(0, 1))
+        z_pass(1, 1, v1, vs1, w4_weights(1, 1))
         g2 = [gather("g20", lodger[0], idx2, U32)]
         for jh in range(2):
             make_h(0, jh)
@@ -206,36 +208,39 @@ def tile_list_homeshare_trio_scores_kernel(
 
         e = [[psum.tile([P, 2, JH], F32, name=f"e{jh}{mp}", tag=f"bank0{2 * jh + mp}") for mp in range(2)] for jh in range(2)]
 
-        def e_pass(b, jh, mp):
+        def e_pass(b, n, jh, mp):
             cols = slice(JH * jh, JH * (jh + 1))
-            for n, (g, gs) in enumerate(((g2[b], g2s), (g3[b], g3s))):
-                for u in range(2):
-                    m0 = P * (2 * mp + u)
-                    nc.tensor.matmul_mx(
-                        out=e[jh][mp][:, u, :],
-                        lhsT=g[:, m0 : m0 + P].bitcast(FP8X4), lhsT_scale=gs[4 * b : P, m0 : m0 + P],
-                        rhs=hq[b][:, cols].bitcast(FP8X4), rhs_scale=hs[b][:, cols],
-                        start=(b == 0 and n == 0 and u == 0), stop=(b == 1 and n == 1 and u == 1),
-                    )
+            g, gs = ((g2[b], g2s), (g3[b], g3s))[n]
+            for u in range(2):
+                m0 = P * (2 * mp + u)
+                nc.tensor.matmul_mx(
+                    out=e[jh][mp][:, u, :],
+                    lhsT=g[:, m0 : m0 + P].bitcast(FP8X4), lhsT_scale=gs[4 * b : P, m0 : m0 + P],
+                    rhs=hq[b][:, cols].bitcast(FP8X4), rhs_scale=hs[b][:, cols],
+                    start=(b == 0 and n == 0 and u == 0), stop=(b == 1 and n == 1 and u == 1),
+                )
 
-        for jh in range(2):
-            for mp in range(2):
-                e_pass(0, jh, mp)
         z_pass(3, 1, v3, vs[12:P, :], w1_weights(1, 1))
+        for n in range(2):
+            for jh in range(2):
+                for mp in range(2):
+                    e_pass(0, n, jh, mp)
         g2.append(gather("g21", lodger[1], idx2, U32))
-        g3.append(gather("g31", volunteer[1], idx3, U32))
+        g3.append(gather("g31", volunteer[1], idx3, U32, tag="w1bf11"))
         for jh in range(2):
             make_h(1, jh)
         for jh in range(2):
             for mp in range(2):
-                e_pass(1, jh, mp)
+                for n in range(2):
+                    e_pass(1, n, jh, mp)
                 th = tile(f"th{jh}{mp}", [P, 2, JH], F32)
                 res = tile(f"res{jh}{mp}", [P, 2, JH], F32)
                 for u in range(2):
                     c = 2 * mp + u
                     nc.scalar.activation(th[:, u, :], e[jh][mp][:, u, :], ACT.Tanh, bias=lean_sb[:, c : c + 1])
-                    nc.vector.tensor_scalar(
-                        res[:, u, :], th[:, u, :], weight_sb[:, c : c + 1], None, ALU.mult
-                    )
+                    if jh == 0:
+                        nc.scalar.activation(res[:, u, :], th[:, u, :], ACT.Identity, scale=weight_sb[:, c : c + 1])
+                    else:
+                        nc.vector.tensor_scalar(res[:, u, :], th[:, u, :], weight_sb[:, c : c + 1], None, ALU.mult)
                 rows = out[2 * P * mp : 2 * P * (mp + 1), JH * jh : JH * (jh + 1)]
                 nc.sync.dma_start(rows.rearrange("(u p) j -> p u j", p=P), res[:])

@@ -18,7 +18,6 @@ PACK = 4
 K_PASS = P * PACK
 T, H, S, T3, S2 = 2048, 1024, 512, 1024, 512
 BLOCKS = H // K_PASS
-JQ = 128
 JH = 256
 
 FLOPS = 2 * 2048 * H * S + 2 * 2 * H * S2 * S
@@ -76,27 +75,31 @@ def tile_list_homeshare_trio_scores_kernel(
             return g
 
         tabs_raw = zeroed("tabs_raw", [P, T])
-        t2s_raw = zeroed("t2s_raw", [P, T3])
         t3s_raw = zeroed("t3s_raw", [P, T3])
         w4s_raw = zeroed("w4s_raw", [P, 2 * H])
+        t2s_raw = zeroed("t2s_raw", [P, T3])
         vs1 = zeroed("vs1", [P, S])
+        warm = tile("warm", [P, 2], F32)
+        nc.vector.memset(warm[:, 0:1], 0.0)
+        nc.scalar.activation(warm[:, 1:2], warm[:, 0:1], ACT.Silu)
 
         w4_raw = tile("w4_raw", [P, 2, 2 * H], U8)
         nc.sync.dma_start(w4_raw[:].bitcast(I32), w4_words.rearrange("a p c -> p a c").bitcast(I32))
         idx = load_list("idx", offs)
-        tab = [load_words("tab0", tab_words[0])]
         load_packed_scales(nc.sync, tabs_raw, tab_scales)
+        tab = [load_words("tab0", tab_words[0])]
+        idx2 = load_list("idx2", offs2)
         w1_raw = {}
         w1_raw[0, 0] = [load_w1(0, 0, 0, 1)]
-        idx2 = load_list("idx2", offs2)
-        idx3 = load_list("idx3", offs3)
-        tab.append(load_words("tab1", tab_words[1]))
         for q in range(4):
             nc.sync.dma_start(
                 w4s_raw[32 * q : 32 * q + 4, :].rearrange("p (a c) -> p a c", a=2).bitcast(I32),
                 w4_scales[:, 4 * q : 4 * q + 4, :].rearrange("a r c -> r a c").bitcast(I32),
             )
+        idx3 = load_list("idx3", offs3)
+        tab.append(load_words("tab1", tab_words[1]))
         w1_raw[1, 0] = [load_w1(1, 0, 0, 1)]
+        load_packed_scales(nc.sync, t2s_raw, tab2_scales)
         tab.append(load_words("tab2", tab_words[2]))
         tab.append(load_words("tab3", tab_words[3]))
         gain_sb = tile("gain_sb", [P, BLOCKS, PACK], F32)
@@ -114,7 +117,6 @@ def tile_list_homeshare_trio_scores_kernel(
             nc.sync.dma_start(weight_sb[:], weight.rearrange("(c p) -> p c", p=P))
 
 
-        load_packed_scales(nc.gpsimd, t2s_raw, tab2_scales)
         load_packed_scales(nc.gpsimd, t3s_raw, tab3_scales)
 
         def deal_columns(name, raw, b, dtype):
@@ -125,25 +127,27 @@ def tile_list_homeshare_trio_scores_kernel(
 
         w4_u16 = w4_raw[:].rearrange("p a c -> p (a c)").bitcast(U16)
         w4 = [deal_columns(f"w4_{b}", w4_u16, b, U16) for b in range(BLOCKS)]
-        v0 = gather("v0", tab[0], idx, U32)
         vs = gather("vs", tabs_raw, idx, U8)
         nc.gpsimd.dma_start(vs1[0:100, :].bitcast(I32), vs[4:104, :].bitcast(I32))
-        g2s = gather("g2s", t2s_raw, idx2, U8, tag="tabs_raw")
-        g3s = gather("g3s", t3s_raw, idx3, U8, tag="t2s_raw")
-        v1 = gather("v1", tab[1], idx, U32)
+        v0 = gather("v0", tab[0], idx, U32)
         w4s = [deal_columns(f"w4s_{b}", w4s_raw[:], b, U8) for b in range(BLOCKS)]
+        v1 = gather("v1", tab[1], idx, U32)
+        g3s = gather("g3s", t3s_raw, idx3, U8, tag="tab1")
 
-        z = [[psum.tile([P, PACK, JQ], F32, name=f"z{b}{q}", tag=f"bank{b}{q}") for q in range(4)] for b in range(BLOCKS)]
+        def z_banks(b):
+            return [[psum.tile([P, 2, JH], F32, name=f"z{b}{jh}{tp}", tag=f"bank{jh}{tp}") for tp in range(2)] for jh in range(2)]
+
+        z = [z_banks(0)]
 
         def z_pass(a, b, v, v_scale, weights):
-            for q in range(4):
-                cols = slice(JQ * q, JQ * (q + 1))
+            for jh in range(2):
+                cols = slice(JH * jh, JH * (jh + 1))
                 for t in range(PACK):
                     lhs, lhs_scale = weights(t)
                     nc.tensor.matmul_mx(
-                        out=z[b][q][:, t, :], lhsT=lhs, lhsT_scale=lhs_scale,
+                        out=z[b][jh][t // 2][:, t % 2, :], lhsT=lhs, lhsT_scale=lhs_scale,
                         rhs=v[:, cols].bitcast(FP8X4), rhs_scale=v_scale[:, cols],
-                        start=(a == 0 and t == 0), stop=(a == 3 and t == PACK - 1),
+                        start=(a == 0 and t % 2 == 0), stop=(a == 3 and t % 2 == 1),
                     )
 
         def w4_weights(a, b):
@@ -177,70 +181,73 @@ def tile_list_homeshare_trio_scores_kernel(
         hs = [tile(f"hs{b}", [P, S], U8) for b in range(BLOCKS)]
 
         def make_h(b, jh):
-            hb = tile(f"hb{b}{jh}", [P, 2, JQ, PACK], BF16)
-            for u in range(2):
-                q = 2 * jh + u
-                act = tile(f"silu{b}{q}", [P, JQ, PACK], F32)
-                nc.scalar.activation(act[:], z[b][q][:].rearrange("p t j -> p j t"), ACT.Silu)
-                nc.vector.tensor_tensor(
-                    hb[:, u, :, :], act[:], gain_sb[:, b, :].unsqueeze(1).to_broadcast([P, JQ, PACK]), ALU.mult
-                )
+            act = tile(f"silu{b}{jh}", [P, 2, JH, 2], F32)
+            for tp in range(2):
+                nc.scalar.activation(act[:, tp, :, :], z[b][jh][tp][:].rearrange("p u j -> p j u"), ACT.Silu)
+            hb = tile(f"hb{b}{jh}", [P, JH, 2, 2], BF16)
+            factor = gain_sb[:, b, :].rearrange("p (tp u) -> p tp u", u=2).unsqueeze(1).to_broadcast([P, JH, 2, 2])
+            nc.vector.tensor_tensor(hb[:], act[:].rearrange("p tp j u -> p j tp u"), factor, ALU.mult)
             cols = slice(JH * jh, JH * (jh + 1))
             nc.vector.quantize_mx(
-                out=hq[b][:, cols].bitcast(FP8X4), scales=hs[b][:, cols], in_=hb[:].rearrange("p u j t -> p (u j t)")
+                out=hq[b][:, cols].bitcast(FP8X4), scales=hs[b][:, cols], in_=hb[:].rearrange("p j tp u -> p (j tp u)")
             )
 
         z_pass(0, 0, v0, vs, w4_weights(0, 0))
         z_pass(1, 0, v1, vs1, w4_weights(1, 0))
         w1_00 = w1_weights(0, 0)
+        g2s = gather("g2s", t2s_raw, idx2, U8)
         w1_10 = w1_weights(1, 0)
         v2 = gather("v2", tab[2], idx, U32)
         z_pass(2, 0, v2, vs[8:P, :], w1_00)
         v3 = gather("v3", tab[3], idx, U32, pieces=2)
         z_pass(3, 0, v3, vs[12:P, :], w1_10)
-        z_pass(0, 1, v0, vs, w4_weights(0, 1))
-        z_pass(1, 1, v1, vs1, w4_weights(1, 1))
         g2 = [gather("g20", lodger[0], idx2, U32)]
         for jh in range(2):
             make_h(0, jh)
+        z.append(z_banks(1))
+        z_pass(0, 1, v0, vs, w4_weights(0, 1))
+        z_pass(1, 1, v1, vs1, w4_weights(1, 1))
         g3 = [gather("g30", volunteer[0], idx3, U32)]
         z_pass(2, 1, v2, vs[8:P, :], w1_weights(0, 1))
 
-        e = [[psum.tile([P, 2, JH], F32, name=f"e{jh}{mp}", tag=f"bank0{2 * jh + mp}") for mp in range(2)] for jh in range(2)]
+        pairs = [psum.tile([P, 2, JH], F32, name=f"e0{mp}", tag=f"bank0{mp}") for mp in range(2)]
+        singles = [psum.tile([P, JH], F32, name=f"e1{c}", tag=f"spare{c}") for c in range(4)]
 
-        def e_pass(b, n, jh, mp):
+        def e_pass(b, n, jh, c):
             cols = slice(JH * jh, JH * (jh + 1))
             g, gs = ((g2[b], g2s), (g3[b], g3s))[n]
-            for u in range(2):
-                m0 = P * (2 * mp + u)
-                nc.tensor.matmul_mx(
-                    out=e[jh][mp][:, u, :],
-                    lhsT=g[:, m0 : m0 + P].bitcast(FP8X4), lhsT_scale=gs[4 * b : P, m0 : m0 + P],
-                    rhs=hq[b][:, cols].bitcast(FP8X4), rhs_scale=hs[b][:, cols],
-                    start=(b == 0 and n == 0 and u == 0), stop=(b == 1 and n == 1 and u == 1),
-                )
+            first, last = (c % 2 == 0, c % 2 == 1) if jh == 0 else (True, True)
+            nc.tensor.matmul_mx(
+                out=pairs[c // 2][:, c % 2, :] if jh == 0 else singles[c][:],
+                lhsT=g[:, P * c : P * (c + 1)].bitcast(FP8X4), lhsT_scale=gs[4 * b : P, P * c : P * (c + 1)],
+                rhs=hq[b][:, cols].bitcast(FP8X4), rhs_scale=hs[b][:, cols],
+                start=(b == 0 and n == 0 and first), stop=(b == 1 and n == 1 and last),
+            )
 
         z_pass(3, 1, v3, vs[12:P, :], w1_weights(1, 1))
-        for n in range(2):
-            for jh in range(2):
-                for mp in range(2):
-                    e_pass(0, n, jh, mp)
+        for jh in (1, 0):
+            for n in range(2):
+                for c in range(4):
+                    e_pass(0, n, jh, c)
         g2.append(gather("g21", lodger[1], idx2, U32))
         g3.append(gather("g31", volunteer[1], idx3, U32, tag="w1bf11"))
         for jh in range(2):
             make_h(1, jh)
         for jh in range(2):
             for mp in range(2):
-                for n in range(2):
-                    e_pass(1, n, jh, mp)
+                for c in (2 * mp, 2 * mp + 1):
+                    for n in range(2):
+                        e_pass(1, n, jh, c)
                 th = tile(f"th{jh}{mp}", [P, 2, JH], F32)
-                res = tile(f"res{jh}{mp}", [P, 2, JH], F32)
+                tag = ("silu11", "hb11")[mp] if jh == 0 else f"res{mp}"
+                res = sb.tile([P, 2, JH], F32, name=f"res{jh}{mp}", tag=tag, align_bytes=64)
                 for u in range(2):
                     c = 2 * mp + u
-                    nc.scalar.activation(th[:, u, :], e[jh][mp][:, u, :], ACT.Tanh, bias=lean_sb[:, c : c + 1])
-                    if jh == 0:
-                        nc.scalar.activation(res[:, u, :], th[:, u, :], ACT.Identity, scale=weight_sb[:, c : c + 1])
-                    else:
-                        nc.vector.tensor_scalar(res[:, u, :], th[:, u, :], weight_sb[:, c : c + 1], None, ALU.mult)
-                rows = out[2 * P * mp : 2 * P * (mp + 1), JH * jh : JH * (jh + 1)]
-                nc.sync.dma_start(rows.rearrange("(u p) j -> p u j", p=P), res[:])
+                    src = pairs[mp][:, u, :] if jh == 0 else singles[c][:]
+                    nc.scalar.activation(th[:, u, :], src, ACT.Tanh, bias=lean_sb[:, c : c + 1])
+                    nc.vector.tensor_scalar(res[:, u, :], th[:, u, :], weight_sb[:, c : c + 1], None, ALU.mult)
+                    if jh == 1:
+                        nc.sync.dma_start(out[P * c : P * (c + 1), JH:S], res[:, u, :])
+                if jh == 0:
+                    rows = out[2 * P * mp : 2 * P * (mp + 1), 0:JH]
+                    nc.sync.dma_start(rows.rearrange("(u p) j -> p u j", p=P), res[:])

@@ -160,7 +160,8 @@ def tile_list_homeshare_trio_scores_kernel(
             pieces = w1_raw[a, b]
             mw = P // len(pieces)
             for h, raw in enumerate(pieces):
-                nc.scalar.copy(
+                copy = nc.scalar.copy if h == 0 else nc.vector.tensor_copy
+                copy(
                     grouped[:, :, mw * h : mw * (h + 1), :].rearrange("p t m i -> p m i t"),
                     raw[:].rearrange("p i (m t) -> p m i t", t=PACK),
                 )
@@ -229,7 +230,7 @@ def tile_list_homeshare_trio_scores_kernel(
             for n in range(2):
                 for c in range(4):
                     e_pass(0, n, jh, c)
-        g2.append(gather("g21", lodger[1], idx2, U32))
+        g2.append(gather("g21", lodger[1], idx2, U32, tag="w1raw111"))
         g3.append(gather("g31", volunteer[1], idx3, U32, tag="w1bf11"))
         for jh in range(2):
             make_h(1, jh)

from contextlib import ExitStack

import concourse.mybir as mybir

F32 = mybir.dt.float32
BF16 = mybir.dt.bfloat16
I32 = mybir.dt.int32
U32 = mybir.dt.uint32
U16 = mybir.dt.uint16
U8 = mybir.dt.uint8
FP8X4 = mybir.dt.float8_e4m3fn_x4
FP4X4 = mybir.dt.float4_e2m1fn_x4
ACT = mybir.ActivationFunctionType
ALU = mybir.AluOpType

P = 128
PACK = 4
K_PASS = P * PACK
T, H, S, T3, S2 = 2048, 1024, 512, 1024, 512
BLOCKS = H // K_PASS
JH = 256

FLOPS = 2 * 2048 * H * S + 2 * 2 * H * S2 * S


def tile_list_homeshare_trio_scores_kernel(
    tc, tab_words, tab_scales, tab2_words, tab2_scales, tab3_words, tab3_scales,
    offs, offs2, offs3, w4_words, w4_scales, w1, gain, lean, weight, out,
):
    nc = tc.nc
    with ExitStack() as ctx:
        sb = ctx.enter_context(tc.tile_pool(name="sb", bufs=1))
        psum = ctx.enter_context(tc.psum_pool(name="psum", bufs=1))

        def tile(name, shape, dtype):
            return sb.tile(shape, dtype, name=name, align_bytes=64)

        def zeroed(name, shape):
            t = tile(name, shape, U8)
            nc.vector.memset(t[:].bitcast(I32), 0)
            return t

        def load_list(name, src):
            t = sb.tile([P, S // 16], U16, name=name)
            nc.sync.dma_start(t[:], src)
            return t

        def load_words(name, src):
            t = tile(name, [P, src.shape[1]], U32)
            nc.sync.dma_start(t[:].bitcast(I32), src.rearrange("p n t -> p (n t)").bitcast(I32))
            return t

        def load_packed_scales(queue, dst, src):
            passes = src.shape[0]
            for q in range(4):
                queue.dma_start(
                    dst[32 * q : 32 * q + 4 * passes, :].bitcast(I32),
                    src[:, 4 * q : 4 * q + 4, :].bitcast(I32),
                )

        def load_w1(a, b, h, n):
            width = K_PASS // n
            t = tile(f"w1raw{a}{b}{h}", [P, PACK, width], F32)
            c0 = K_PASS * b + width * h
            rows = w1[K_PASS * a : K_PASS * (a + 1), c0 : c0 + width]
            nc.sync.dma_start(t[:], rows.rearrange("(p i) c -> p i c", i=PACK))
            return t

        def gather(name, window, lst, dtype, tag=None, pieces=1):
            g = sb.tile([P, S], dtype, name=name, tag=tag or name, align_bytes=64)
            n = S // pieces
            for h in range(pieces):
                offsets = lst[:, n // 16 * h : n // 16 * (h + 1)]
                nc.vector.tensor_copy(g[:, n * h : n * (h + 1)], window[:].indirect(offsets))
            return g

        tabs_raw = zeroed("tabs_raw", [P, T])
        t3s_raw = zeroed("t3s_raw", [P, T3])
        w4s_raw = zeroed("w4s_raw", [P, 2 * H])
        t2s_raw = zeroed("t2s_raw", [P, T3])
        vs1 = zeroed("vs1", [P, S])
        warm = tile("warm", [P, 2], F32)
        nc.vector.memset(warm[:, 0:1], 0.0)
        nc.scalar.activation(warm[:, 1:2], warm[:, 0:1], ACT.Silu)

        w4_raw = tile("w4_raw", [P, 2, 2 * H], U8)
        nc.sync.dma_start(w4_raw[:].bitcast(I32), w4_words.rearrange("a p c -> p a c").bitcast(I32))
        idx = load_list("idx", offs)
        load_packed_scales(nc.sync, tabs_raw, tab_scales)
        tab = [load_words("tab0", tab_words[0])]
        idx2 = load_list("idx2", offs2)
        w1_raw = {}
        w1_raw[0, 0] = [load_w1(0, 0, 0, 1)]
        for q in range(4):
            nc.sync.dma_start(
                w4s_raw[32 * q : 32 * q + 4, :].rearrange("p (a c) -> p a c", a=2).bitcast(I32),
                w4_scales[:, 4 * q : 4 * q + 4, :].rearrange("a r c -> r a c").bitcast(I32),
            )
        idx3 = load_list("idx3", offs3)
        tab.append(load_words("tab1", tab_words[1]))
        w1_raw[1, 0] = [load_w1(1, 0, 0, 1)]
        load_packed_scales(nc.sync, t2s_raw, tab2_scales)
        tab.append(load_words("tab2", tab_words[2]))
        tab.append(load_words("tab3", tab_words[3]))
        gain_sb = tile("gain_sb", [P, BLOCKS, PACK], F32)
        nc.sync.dma_start(gain_sb[:], gain.rearrange("(b p t) -> p b t", p=P, t=PACK))
        lodger = [load_words("lodger0", tab2_words[0])]
        w1_raw[0, 1] = [load_w1(0, 1, 0, 1)]
        volunteer = [load_words("volunteer0", tab3_words[0])]
        w1_raw[1, 1] = [load_w1(1, 1, h, 2) for h in range(2)]
        lodger.append(load_words("lodger1", tab2_words[1]))
        volunteer.append(load_words("volunteer1", tab3_words[1]))
        lean_sb = tile("lean_sb", [P, 4], F32)
        weight_sb = tile("weight_sb", [P, 4], F32)
        with nc.allow_non_contiguous_dma(reason="one value a partition"):
            nc.sync.dma_start(lean_sb[:], lean.rearrange("(c p) -> p c", p=P))
            nc.sync.dma_start(weight_sb[:], weight.rearrange("(c p) -> p c", p=P))


        load_packed_scales(nc.gpsimd, t3s_raw, tab3_scales)

        def deal_columns(name, raw, b, dtype):
            dealt = tile(name, [P, 2, PACK, P], dtype)
            src = raw.rearrange("p (a b m t) -> p a b t m", a=2, b=BLOCKS, t=PACK)
            nc.vector.tensor_copy(dealt[:], src[:, :, b, :, :])
            return dealt

        w4_u16 = w4_raw[:].rearrange("p a c -> p (a c)").bitcast(U16)
        w4 = [deal_columns(f"w4_{b}", w4_u16, b, U16) for b in range(BLOCKS)]
        vs = gather("vs", tabs_raw, idx, U8)
        nc.gpsimd.dma_start(vs1[0:100, :].bitcast(I32), vs[4:104, :].bitcast(I32))
        v0 = gather("v0", tab[0], idx, U32)
        w4s = [deal_columns(f"w4s_{b}", w4s_raw[:], b, U8) for b in range(BLOCKS)]
        v1 = gather("v1", tab[1], idx, U32)
        g3s = gather("g3s", t3s_raw, idx3, U8, tag="tab1")

        def z_banks(b):
            return [[psum.tile([P, 2, JH], F32, name=f"z{b}{jh}{tp}", tag=f"bank{jh}{tp}") for tp in range(2)] for jh in range(2)]

        z = [z_banks(0)]

        def z_pass(a, b, v, v_scale, weights):
            for jh in range(2):
                cols = slice(JH * jh, JH * (jh + 1))
                for t in range(PACK):
                    lhs, lhs_scale = weights(t)
                    nc.tensor.matmul_mx(
                        out=z[b][jh][t // 2][:, t % 2, :], lhsT=lhs, lhsT_scale=lhs_scale,
                        rhs=v[:, cols].bitcast(FP8X4), rhs_scale=v_scale[:, cols],
                        start=(a == 0 and t % 2 == 0), stop=(a == 3 and t % 2 == 1),
                    )

        def w4_weights(a, b):
            def get(t):
                return w4[b][:, a, t, :].bitcast(FP4X4), w4s[b][:, a, t, :]
            return get

        def w1_weights(a, b):
            grouped = tile(f"w1bf{a}{b}", [P, PACK, P, PACK], BF16)
            pieces = w1_raw[a, b]
            mw = P // len(pieces)
            for h, raw in enumerate(pieces):
                copy = nc.scalar.copy if h == 0 else nc.vector.tensor_copy
                copy(
                    grouped[:, :, mw * h : mw * (h + 1), :].rearrange("p t m i -> p m i t"),
                    raw[:].rearrange("p i (m t) -> p m i t", t=PACK),
                )
            codes = tile(f"w1q{a}{b}", [P, K_PASS], U32)
            scales = tile(f"w1s{a}{b}", [P, K_PASS], U8)
            for tp in range(2):
                nc.vector.quantize_mx(
                    out=codes[:, 256 * tp : 256 * (tp + 1)].bitcast(FP8X4),
                    scales=scales[:, 256 * tp : 256 * (tp + 1)],
                    in_=grouped[:, 2 * tp : 2 * tp + 2, :, :].rearrange("p t m i -> p (t m i)"),
                )

            def get(t):
                return codes[:, P * t : P * (t + 1)].bitcast(FP8X4), scales[:, P * t : P * (t + 1)]
            return get

        hq = [tile(f"hq{b}", [P, S], U32) for b in range(BLOCKS)]
        hs = [tile(f"hs{b}", [P, S], U8) for b in range(BLOCKS)]

        def make_h(b, jh):
            act = tile(f"silu{b}{jh}", [P, 2, JH, 2], F32)
            for tp in range(2):
                nc.scalar.activation(act[:, tp, :, :], z[b][jh][tp][:].rearrange("p u j -> p j u"), ACT.Silu)
            hb = tile(f"hb{b}{jh}", [P, JH, 2, 2], BF16)
            factor = gain_sb[:, b, :].rearrange("p (tp u) -> p tp u", u=2).unsqueeze(1).to_broadcast([P, JH, 2, 2])
            nc.vector.tensor_tensor(hb[:], act[:].rearrange("p tp j u -> p j tp u"), factor, ALU.mult)
            cols = slice(JH * jh, JH * (jh + 1))
            nc.vector.quantize_mx(
                out=hq[b][:, cols].bitcast(FP8X4), scales=hs[b][:, cols], in_=hb[:].rearrange("p j tp u -> p (j tp u)")
            )

        z_pass(0, 0, v0, vs, w4_weights(0, 0))
        z_pass(1, 0, v1, vs1, w4_weights(1, 0))
        w1_00 = w1_weights(0, 0)
        g2s = gather("g2s", t2s_raw, idx2, U8)
        w1_10 = w1_weights(1, 0)
        v2 = gather("v2", tab[2], idx, U32)
        z_pass(2, 0, v2, vs[8:P, :], w1_00)
        v3 = gather("v3", tab[3], idx, U32, pieces=2)
        z_pass(3, 0, v3, vs[12:P, :], w1_10)
        g2 = [gather("g20", lodger[0], idx2, U32)]
        for jh in range(2):
            make_h(0, jh)
        z.append(z_banks(1))
        z_pass(0, 1, v0, vs, w4_weights(0, 1))
        z_pass(1, 1, v1, vs1, w4_weights(1, 1))
        g3 = [gather("g30", volunteer[0], idx3, U32)]
        z_pass(2, 1, v2, vs[8:P, :], w1_weights(0, 1))

        pairs = [psum.tile([P, 2, JH], F32, name=f"e0{mp}", tag=f"bank0{mp}") for mp in range(2)]
        singles = [psum.tile([P, JH], F32, name=f"e1{c}", tag=f"spare{c}") for c in range(4)]

        def e_pass(b, n, jh, c):
            cols = slice(JH * jh, JH * (jh + 1))
            g, gs = ((g2[b], g2s), (g3[b], g3s))[n]
            first, last = (c % 2 == 0, c % 2 == 1) if jh == 0 else (True, True)
            nc.tensor.matmul_mx(
                out=pairs[c // 2][:, c % 2, :] if jh == 0 else singles[c][:],
                lhsT=g[:, P * c : P * (c + 1)].bitcast(FP8X4), lhsT_scale=gs[4 * b : P, P * c : P * (c + 1)],
                rhs=hq[b][:, cols].bitcast(FP8X4), rhs_scale=hs[b][:, cols],
                start=(b == 0 and n == 0 and first), stop=(b == 1 and n == 1 and last),
            )

        z_pass(3, 1, v3, vs[12:P, :], w1_weights(1, 1))
        for jh in (1, 0):
            for n in range(2):
                for c in range(4):
                    e_pass(0, n, jh, c)
        g2.append(gather("g21", lodger[1], idx2, U32, tag="w1raw111"))
        g3.append(gather("g31", volunteer[1], idx3, U32, tag="w1bf11"))
        for jh in range(2):
            make_h(1, jh)
        for jh in range(2):
            for mp in range(2):
                for c in (2 * mp, 2 * mp + 1):
                    for n in range(2):
                        e_pass(1, n, jh, c)
                th = tile(f"th{jh}{mp}", [P, 2, JH], F32)
                tag = ("silu11", "hb11")[mp] if jh == 0 else f"res{mp}"
                res = sb.tile([P, 2, JH], F32, name=f"res{jh}{mp}", tag=tag, align_bytes=64)
                for u in range(2):
                    c = 2 * mp + u
                    src = pairs[mp][:, u, :] if jh == 0 else singles[c][:]
                    nc.scalar.activation(th[:, u, :], src, ACT.Tanh, bias=lean_sb[:, c : c + 1])
                    nc.vector.tensor_scalar(res[:, u, :], th[:, u, :], weight_sb[:, c : c + 1], None, ALU.mult)
                    if jh == 1:
                        nc.sync.dma_start(out[P * c : P * (c + 1), JH:S], res[:, u, :])
                if jh == 0:
                    rows = out[2 * P * mp : 2 * P * (mp + 1), 0:JH]
                    nc.sync.dma_start(rows.rearrange("(u p) j -> p u j", p=P), res[:])
